import numpy as np
import ml_dtypes


def mxq(x, axis, fmt="e4m3"):
    dtype, down = {"e4m3": (ml_dtypes.float8_e4m3fn, 7), "e5m2": (ml_dtypes.float8_e5m2, 14)}[fmt]
    v = np.moveaxis(np.asarray(x, np.float32).astype(ml_dtypes.bfloat16).astype(np.float64), axis, -1)
    blocks = v.reshape(v.shape[:-1] + (-1, 32))
    amax = np.abs(blocks).max(-1, keepdims=True)
    byte = np.maximum(np.where(amax > 0, np.frexp(amax)[1] - 1 + 127, 0) - down, 1)
    scale = np.exp2(byte - 127.0)
    codes = (blocks / scale).astype(np.float32).astype(dtype).astype(np.float64)
    return np.moveaxis((codes * scale).reshape(v.shape), -1, axis)


WIDE = False


def mx_kscale(k):
    if not WIDE:
        return np.ones(k)
    levels = np.array([10, -10, 5, -5, 0])
    if k % 512:
        return np.exp2(np.random.permutation(np.resize(levels, k // 32))).repeat(32)
    a = np.empty((k // 512, 16))
    for p in range(k // 512):
        a[p, :8] = np.random.permutation(np.resize(levels, 8))
        for g in range(8):
            far = levels[np.abs(levels - a[p, g]) >= 10]
            a[p, g + 8] = far[np.random.randint(len(far))]
    return np.exp2(a.ravel()).repeat(32)


def f64(x):
    return np.asarray(x).astype(np.float64)


def striped(idx):
    return np.tile(idx.reshape(-1, 16).T, (8, 1)).astype(np.uint16)


def unstriped(offs):
    return offs[:16].T.reshape(-1).astype(np.int64)


def pack_weight(w):
    k, n = w.shape
    w = f64(np.asarray(w, np.float32).astype(ml_dtypes.bfloat16)).reshape(k // 32, 32, n)
    amax = np.abs(w).max(1)
    byte = np.clip(np.where(amax > 0, np.frexp(amax)[1] - 1 + 127 - 7, 1), 1, 254)
    scaled = (w * np.exp2(127.0 - byte)[:, None, :]).reshape(k, n).astype(np.float32)
    words = np.ascontiguousarray(scaled.reshape(k // 512, 128, 4, n).transpose(0, 1, 3, 2)).astype(ml_dtypes.float8_e4m3fn).view(np.uint8)
    return words, np.ascontiguousarray(byte.astype(np.uint8).reshape(k // 512, 16, n))


def unpack_weight(words, scales):
    g, p, n, _ = words.shape
    vals = np.ascontiguousarray(words).view(ml_dtypes.float8_e4m3fn).astype(np.float64) * np.repeat(np.exp2(scales.astype(np.float64) - 127.0), 8, axis=1)[..., None]
    return vals.transpose(0, 1, 3, 2).reshape(g * 512, n)


K, T, S, D, N, H, V, U = 512, 2048, 1024, 4, 128, 512, 256, 512


def setup_inputs():
    n = np.random.standard_normal
    s = mx_kscale(K)[:, None]
    u = mx_kscale(H)
    packed_xT = pack_weight(n((K, T)) * s)
    return {
        "x_words": packed_xT[0],
        "x_scales": packed_xT[1],
        "w1": (n((K, H)) / np.sqrt(K) / s).astype(np.float32),
        "w2": (n((K, H)) / np.sqrt(K) / s).astype(np.float32),
        "off": (n((H, S))).astype(np.float32),
        "sg": (np.random.uniform(0.3, 0.8, (H, S))).astype(np.float32),
        "unit": (np.random.uniform(0.6, 1.4, (H, 1)) * u[:, None]).astype(np.float32),
        "w3": (n((H, N)) / np.sqrt(H) / u[:, None]).astype(np.float32),
        "offs": striped(np.random.permutation(T)[:S]),
        "qry": striped(np.random.permutation(np.concatenate([np.arange(V), np.random.randint(0, V, U - V)]))),
    }


def reference(x_words, x_scales, w1, w2, off, sg, unit, w3, offs, qry):
    xq = unpack_weight(x_words, x_scales)[:, unstriped(offs)]
    py = mxq(f64(w1), 0, "e4m3").T @ xq
    fx = f64(off) - (0.5 * py)
    we0 = np.exp(-1.0 * ((0.6 * fx) ** 2))
    wf = we0 * fx
    m0 = (wf.reshape(len(wf), -1, D).sum(axis=2)) / (we0.reshape(len(we0), -1, D).sum(axis=2) + 0.1)
    res = fx - np.repeat(m0, D, axis=1)
    we1 = we0 * (f64(sg) / (np.abs(res) + f64(sg)))
    wf1 = we1 * fx
    m1 = (wf1.reshape(len(wf1), -1, D).sum(axis=2)) / (we1.reshape(len(we1), -1, D).sum(axis=2) + 0.1)
    mq = m1[:, unstriped(qry)]
    ny = mxq(f64(w2), 0, "e4m3").T @ xq
    nm_ = ny.reshape(len(ny), -1, D).mean(axis=2)
    nq = nm_[:, unstriped(qry)]
    hid = f64(unit) * (mq * np.tanh(nq))
    return mxq(f64(w3), 0, "e4m3").T @ mxq(hid, 0, "e4m3")

@@ -1,0 +1,351 @@
+from contextlib import ExitStack
+
+import concourse.mybir as mybir
+from concourse.masks import make_identity
+
+FLOPS = 1140850688
+
+F32 = mybir.dt.float32
+BF16 = mybir.dt.bfloat16
+I32 = mybir.dt.int32
+U32 = mybir.dt.uint32
+U16 = mybir.dt.uint16
+U8 = mybir.dt.uint8
+FP8X4 = mybir.dt.float8_e4m3fn_x4
+ACT = mybir.ActivationFunctionType
+ALU = mybir.AluOpType
+
+P = 128
+PACK = 4
+K, T, S, D, N, H, V, U = 512, 2048, 1024, 4, 128, 512, 256, 512
+HALF = S // 2
+VH = V // 2
+QUERY_SLICE = 128
+LIST_COLS = 16
+WEIGHT_BANKS = ("bank7", "bank2")
+VALUE_BANKS = ("bank6", "bank3")
+
+
+def tile_picked_yimlsq_nrm_p_kernel(
+    tc, x_words, x_scales, w1, w2, off, sg, unit, w3, offs, qry, out
+):
+    nc = tc.nc
+    with ExitStack() as ctx:
+        lists = ctx.enter_context(tc.tile_pool(name="lists", bufs=1))
+        keep = ctx.enter_context(tc.tile_pool(name="keep", bufs=1))
+        ring = ctx.enter_context(tc.tile_pool(name="ring", bufs=3))
+        psum = ctx.enter_context(tc.psum_pool(name="psum", bufs=1))
+
+        offs_sb = lists.tile([P, S // LIST_COLS], U16, name="offs_sb")
+        qry_sb = lists.tile([P, U // LIST_COLS], U16, name="qry_sb")
+
+        table_words = keep.tile([P, T], I32, name="table_words")
+        table_scales = keep.tile([P, T], U8, name="table_scales")
+        nc.vector.memset(table_scales[:].bitcast(I32), 0)
+
+        def load_weight_half(w, h, name):
+            raw = keep.tile([P, PACK, H // 2], F32, name=name)
+            nc.sync.dma_start(raw[:], w.rearrange("(p j) c -> p j c", j=PACK)[:, :, h * (H // 2) : (h + 1) * (H // 2)])
+            return raw
+
+        def load_rows(src, t, name, pieces=1):
+            rows = keep.tile([P, S], F32, name=name)
+            for i in range(pieces):
+                cols = slice(i * S // pieces, (i + 1) * S // pieces)
+                nc.sync.dma_start(rows[:, cols], src.rearrange("(p t) s -> p t s", t=PACK)[:, t, cols])
+            return rows
+
+        nc.sync.dma_start(offs_sb[:], offs)
+        w1_raw = [load_weight_half(w1, 0, "w1_raw0")]
+        for q in range(4):
+            nc.sync.dma_start(
+                table_scales[32 * q : 32 * q + 4, :].bitcast(I32), x_scales[0][4 * q : 4 * q + 4, :].bitcast(I32)
+            )
+        w1_raw.append(load_weight_half(w1, 1, "w1_raw1"))
+        nc.sync.dma_start(table_words[:], x_words[0].rearrange("p c r -> p (c r)").bitcast(I32))
+        w2_raw = [load_weight_half(w2, h, "w2_raw%d" % h) for h in range(2)]
+        off_sb = [load_rows(off, 0, "off0", pieces=2)]
+        off_sb.extend(load_rows(off, t, "off%d" % t) for t in range(1, PACK))
+        sg_sb = [load_rows(sg, t, "sg%d" % t) for t in range(PACK)]
+        w3_raw = keep.tile([P, PACK, N], F32, name="w3_raw")
+        nc.sync.dma_start(w3_raw[:], w3.rearrange("(p j) n -> p j n", j=PACK))
+        unit_sb = keep.tile([P, PACK], F32, name="unit_sb")
+        nc.sync.dma_start(unit_sb[:], unit.rearrange("(p t) o -> p (t o)", t=PACK))
+        nc.sync.dma_start(qry_sb[:], qry)
+
+        ident = keep.tile([P, P], F32, name="ident")
+        make_identity(nc, ident[:])
+
+        def round_weight(raw_halves, name):
+            grouped = keep.tile([P, PACK, P, PACK], BF16, name=name, align_bytes=64)
+            for h in range(2):
+                nc.scalar.activation(
+                    out=grouped[:, :, h * (P // 2) : (h + 1) * (P // 2), :].rearrange("p t m j -> p m t j"),
+                    in_=raw_halves[h][:].rearrange("p j (m t) -> p m t j", t=PACK),
+                    func=ACT.Copy,
+                )
+            return grouped[:].rearrange("p t m j -> p (t m j)")
+
+        def quantize(grouped, name):
+            width = grouped.shape[1] // PACK
+            codes = keep.tile([P, width], U32, name=name + "_codes", align_bytes=64)
+            scales = keep.tile([P, width], U8, name=name + "_scales", align_bytes=64)
+            nc.vector.quantize_mx(out=codes[:].bitcast(FP8X4), scales=scales[:], in_=grouped)
+            return codes, scales
+
+        picked_scales = keep.tile([P, S], U8, name="picked_scales")
+        nc.vector.tensor_copy(picked_scales[:], table_scales[:].indirect(offs_sb[:]))
+        dealt_scales = keep.tile([P, S], U8, name="dealt_scales", align_bytes=64)
+        nc.vector.tensor_copy(
+            dealt_scales[:].rearrange("p (h d v) -> p h d v", h=2, d=D),
+            picked_scales[:].rearrange("p (h v d) -> p h d v", h=2, d=D),
+        )
+        x_scale = [dealt_scales[:, vh * HALF : (vh + 1) * HALF] for vh in range(2)]
+        w1_codes, w1_scales = quantize(round_weight(w1_raw, "w1_grouped"), "w1")
+        x_code = []
+        for vh in range(2):
+            words = keep.tile([P, HALF], U32, name="picked_words%d" % vh, align_bytes=64)
+            cols = HALF // LIST_COLS
+            nc.vector.tensor_copy(
+                words[:].rearrange("p (d v) -> p v d", d=D),
+                table_words[:].bitcast(U32).indirect(offs_sb[:, vh * cols : (vh + 1) * cols]),
+            )
+            x_code.append(words)
+
+        chunks = [(t, vh) for t in range(PACK) for vh in range(2)]
+        last = len(chunks) - 1
+
+        def feature_cols(t):
+            return slice(t * P, (t + 1) * P)
+
+        def paired(tile_ap):
+            return tile_ap.rearrange("p (a v b) -> p a v b", a=2, b=2)
+
+        def given(rows, vh):
+            return rows[:, vh * HALF : (vh + 1) * HALF].rearrange("p (v a b) -> p a v b", a=2, b=2)
+
+        def group_sums(bank, slot, values):
+            for d in range(D):
+                first = (d // 2) * 2 * VH + d % 2
+                nc.tensor.matmul(
+                    bank[:, slot * P : (slot + 1) * P],
+                    lhsT=values[:, first : first + 2 * VH - d % 2 : 2],
+                    rhs=ident[:],
+                    is_transpose=True,
+                    start=(d == 0),
+                    stop=(d == D - 1),
+                )
+
+        fx = [keep.tile([P, HALF], F32, name="fx%d" % c) for c in range(len(chunks))]
+        we0 = [keep.tile([P, HALF], F32, name="we0_%d" % c) for c in range(len(chunks))]
+        tanh_nm = [keep.tile([P, 2 * V], F32, name="tanh_nm%d" % i) for i in range(2)]
+        last_square = keep.tile([P, HALF], F32, name="last_square")
+        weight_sums0 = {}
+        value_sums0 = {}
+
+        def offsets_of(c):
+            t, vh = chunks[c]
+            tag = "bank%d" % (c % 6)
+            py = psum.tile([P, HALF], F32, name="py%d" % c, tag=tag)
+            nc.tensor.matmul_mx(
+                py[:],
+                lhsT=w1_codes[:, feature_cols(t)].bitcast(FP8X4),
+                lhsT_scale=w1_scales[:, feature_cols(t)],
+                rhs=x_code[vh][:].bitcast(FP8X4),
+                rhs_scale=x_scale[vh],
+                start=True,
+                stop=True,
+            )
+            py_view = py[:].rearrange("p (a b v) -> p a v b", a=2, b=2)
+            for a in range(2):
+                nc.vector.scalar_tensor_tensor(
+                    out=paired(fx[c][:])[:, a],
+                    in0=py_view[:, a],
+                    scalar=-0.5,
+                    in1=given(off_sb[t], vh)[:, a],
+                    op0=ALU.mult,
+                    op1=ALU.add,
+                )
+
+        def first_weights(c):
+            if c == last:
+                square = last_square
+            else:
+                square = ring.tile([P, HALF], F32, name="square", tag="square")
+            nc.scalar.activation(out=square[:], in_=fx[c][:], func=ACT.Square, scale=0.6)
+            nc.scalar.activation(out=we0[c][:], in_=square[:], func=ACT.Exp, scale=-1.0)
+
+        wf = [keep.tile([P, HALF], F32, name="wf%d" % c) for c in range(len(chunks))]
+
+        def weighted_offsets(c):
+            nc.vector.tensor_tensor(out=wf[c][:], in0=we0[c][:], in1=fx[c][:], op=ALU.mult)
+
+        def first_sums(c):
+            if c % 4 == 0:
+                weight_sums0[c // 4] = psum.tile([P, 4 * P], F32, name="s0", tag=WEIGHT_BANKS[c // 4])
+                value_sums0[c // 4] = psum.tile([P, 4 * P], F32, name="n0", tag=VALUE_BANKS[c // 4])
+            group_sums(weight_sums0[c // 4], c % 4, we0[c])
+            group_sums(value_sums0[c // 4], c % 4, wf[c])
+
+        def normals(w2_codes, w2_scales):
+            for i in range(2):
+                bank = psum.tile([P, 2 * V], F32, name="normal%d" % i, tag="bank%d" % (6 + i))
+                for s in range(4):
+                    t, vh = 2 * i + s // 2, s % 2
+                    for d in range(D):
+                        nc.tensor.matmul_mx(
+                            bank[:, s * VH : (s + 1) * VH],
+                            lhsT=w2_codes[:, feature_cols(t)].bitcast(FP8X4),
+                            lhsT_scale=w2_scales[:, feature_cols(t)],
+                            rhs=x_code[vh][:, d * VH : (d + 1) * VH].bitcast(FP8X4),
+                            rhs_scale=x_scale[vh][:, d * VH : (d + 1) * VH],
+                            start=(d == 0),
+                            stop=(d == D - 1),
+                        )
+                nc.scalar.activation(out=tanh_nm[i][:], in_=bank[:], func=ACT.Tanh, scale=1.0 / D)
+
+        w2_grouped = round_weight(w2_raw, "w2_grouped")
+        for step in range(len(chunks) + 1):
+            if step == 6:
+                normals(*quantize(w2_grouped, "w2"))
+            if step < len(chunks):
+                offsets_of(step)
+            if step >= 1:
+                first_weights(step - 1)
+        for c in range(len(chunks)):
+            weighted_offsets(c)
+        for c in range(4):
+            first_sums(c)
+
+        def group_mean(weight_sums, value_sums, inverse, turned):
+            width = inverse.shape[1]
+            squared = ring.tile([P, width], F32, name="squared", tag="squared")
+            nc.scalar.activation(out=squared[:], in_=weight_sums, func=ACT.Square, bias=0.1)
+            nc.scalar.activation(out=inverse, in_=squared[:], func=ACT.Abs_reciprocal_sqrt)
+            mean = ring.tile([P, width], F32, name="mean", tag="mean")
+            nc.vector.tensor_tensor(out=mean[:], in0=value_sums, in1=inverse, op=ALU.mult)
+            for s in range(width // P):
+                nc.tensor.transpose(turned[:, s * P : (s + 1) * P], mean[:, s * P : (s + 1) * P], ident[:])
+
+        scaled = [keep.tile([P, HALF], F32, name="scaled%d" % c) for c in range(len(chunks))]
+        cells = [keep.tile([P, V], F32, name="cells%d" % t) for t in range(PACK)]
+        m0 = {}
+        m1 = {}
+        size = {}
+        inverse_size = {}
+        weight_sums1 = {}
+        value_sums1 = {}
+        picked_hid = keep.tile([P, PACK, U], BF16, name="picked_hid")
+
+        def first_mean(i):
+            m0[i] = psum.tile([P, 4 * VH], F32, name="m0_%d" % i, tag="bank%d" % (4 + i))
+            if i == 0:
+                inverse = last_square
+            else:
+                inverse = ring.tile([P, HALF], F32, name="inverse", tag="inverse")
+            group_mean(weight_sums0[i][:], value_sums0[i][:], inverse[:], m0[i])
+
+        def scale_weights(c):
+            t, vh = chunks[c]
+            nc.vector.tensor_tensor(
+                out=paired(scaled[c][:]), in0=paired(we0[c][:]), in1=given(sg_sb[t], vh), op=ALU.mult
+            )
+
+        def residual(c):
+            res = ring.tile([P, HALF], F32, name="res", tag="res")
+            mean = m0[c // 4][:, (c % 4) * VH : (c % 4 + 1) * VH]
+            spread = mean.unsqueeze(1).unsqueeze(3).to_broadcast([P, 2, VH, 2])
+            nc.vector.tensor_tensor(out=paired(res[:]), in0=paired(fx[c][:]), in1=spread, op=ALU.subtract)
+            size[c] = ring.tile([P, HALF], F32, name="size", tag="size")
+            nc.scalar.activation(out=size[c][:], in_=res[:], func=ACT.Abs)
+
+        def denominators(c):
+            t, vh = chunks[c]
+            denom = ring.tile([P, HALF], F32, name="denom", tag="denom")
+            nc.vector.tensor_tensor(out=paired(denom[:]), in0=paired(size[c][:]), in1=given(sg_sb[t], vh), op=ALU.add)
+            denom_sq = ring.tile([P, HALF], F32, name="denom_sq", tag="denom_sq")
+            nc.scalar.activation(out=denom_sq[:], in_=denom[:], func=ACT.Square)
+            inverse_size[c] = ring.tile([P, HALF], F32, name="inverse_size", tag="inverse_size")
+            nc.scalar.activation(out=inverse_size[c][:], in_=denom_sq[:], func=ACT.Abs_reciprocal_sqrt)
+
+        def second_sums(c):
+            t, vh = chunks[c]
+            if vh == 0:
+                weight_sums1[t] = psum.tile([P, V], F32, name="s1_%d" % t, tag=WEIGHT_BANKS[t % 2])
+                value_sums1[t] = psum.tile([P, V], F32, name="n1_%d" % t, tag=VALUE_BANKS[t % 2])
+            we1 = ring.tile([P, HALF], F32, name="we1", tag="we1")
+            nc.vector.tensor_tensor(out=we1[:], in0=scaled[c][:], in1=inverse_size[c][:], op=ALU.mult)
+            wf1 = ring.tile([P, HALF], F32, name="wf1", tag="wf")
+            nc.vector.tensor_tensor(out=wf1[:], in0=we1[:], in1=fx[c][:], op=ALU.mult)
+            group_sums(weight_sums1[t], vh, we1)
+            group_sums(value_sums1[t], vh, wf1)
+
+        def hidden(t, first, count):
+            if first == 0:
+                m1[t] = psum.tile([P, V], F32, name="m1_%d" % t, tag="bank%d" % (t % 2))
+            cols = slice(first, first + count)
+            inverse = ring.tile([P, count], F32, name="inverse", tag="inverse")
+            group_mean(weight_sums1[t][:, cols], value_sums1[t][:, cols], inverse[:], m1[t][:, cols])
+            nc.vector.scalar_tensor_tensor(
+                out=cells[t][:, cols],
+                in0=m1[t][:, cols],
+                scalar=unit_sb[:, t : t + 1],
+                in1=tanh_nm[t // 2][:, (t % 2) * V + first : (t % 2) * V + first + count],
+                op0=ALU.mult,
+                op1=ALU.mult,
+            )
+
+        def look_up(t, s, on_vector):
+            cols = QUERY_SLICE // LIST_COLS
+            picked = picked_hid[:, t, s * QUERY_SLICE : (s + 1) * QUERY_SLICE]
+            window = cells[t][:].indirect(qry_sb[:, s * cols : (s + 1) * cols])
+            if on_vector:
+                nc.vector.tensor_copy(picked, window)
+            else:
+                nc.scalar.activation(out=picked, in_=window, func=ACT.Copy)
+
+        first_mean(0)
+        for c in range(4, len(chunks)):
+            first_sums(c)
+        first_mean(1)
+        for step in range(len(chunks) + 3):
+            if step < len(chunks):
+                residual(step)
+            if 0 <= step - 1 < len(chunks):
+                denominators(step - 1)
+                scale_weights(step - 1)
+            if step == last + 2:
+                hidden(PACK - 1, 0, VH)
+            if 0 <= step - 2 < len(chunks):
+                second_sums(step - 2)
+            if step in (4, 6, 8):
+                hidden(step // 2 - 2, 0, V)
+        hidden(PACK - 1, VH, VH)
+        for t in range(PACK):
+            for s in range(U // QUERY_SLICE):
+                look_up(t, s, t == PACK - 1 and s % 2 == 0)
+
+        w3_grouped = keep.tile([P, N, PACK], BF16, name="w3_grouped", align_bytes=64)
+        nc.scalar.activation(out=w3_grouped[:], in_=w3_raw[:].rearrange("p j n -> p n j"), func=ACT.Copy)
+        w3_codes, w3_scales = quantize(w3_grouped[:].rearrange("p n j -> p (n j)"), "w3")
+        for h in range(2):
+            queries = slice(h * (U // 2), (h + 1) * (U // 2))
+            hid = keep.tile([P, U // 2, PACK], BF16, name="hid%d" % h, align_bytes=64)
+            nc.vector.tensor_copy(
+                hid[:].rearrange("p (c i) t -> p c t i", i=4),
+                picked_hid[:, :, queries].rearrange("p t (c i) -> p c t i", i=4),
+            )
+            hid_codes, hid_scales = quantize(hid[:].rearrange("p r t -> p (r t)"), "hid%d" % h)
+            patches = psum.tile([P, U // 2], F32, name="patches%d" % h, tag="bank%d" % (4 + h))
+            nc.tensor.matmul_mx(
+                patches[:],
+                lhsT=w3_codes[:].bitcast(FP8X4),
+                lhsT_scale=w3_scales[:],
+                rhs=hid_codes[:].bitcast(FP8X4),
+                rhs_scale=hid_scales[:],
+                start=True,
+                stop=True,
+            )
+            result = keep.tile([P, U // 2], F32, name="result%d" % h)
+            nc.scalar.copy(result[:], patches[:])
+            nc.sync.dma_start(out[:, queries], result[:])

@@ -22,6 +22,7 @@ HALF = S // 2
 VH = V // 2
 QUERY_SLICE = 128
 LIST_COLS = 16
+W1_PIECES = 4
 WEIGHT_BANKS = ("bank7", "bank2")
 VALUE_BANKS = ("bank6", "bank3")
 
@@ -43,47 +44,48 @@ def tile_picked_yimlsq_nrm_p_kernel(
         table_scales = keep.tile([P, T], U8, name="table_scales")
         nc.vector.memset(table_scales[:].bitcast(I32), 0)
 
-        def load_weight_half(w, h, name):
-            raw = keep.tile([P, PACK, H // 2], F32, name=name)
-            nc.sync.dma_start(raw[:], w.rearrange("(p j) c -> p j c", j=PACK)[:, :, h * (H // 2) : (h + 1) * (H // 2)])
+        def load_weight_piece(w, i, pieces, name):
+            width = H // pieces
+            raw = keep.tile([P, PACK, width], F32, name="%s%d" % (name, i), align_bytes=64)
+            nc.sync.dma_start(raw[:], w.rearrange("(p j) c -> p j c", j=PACK)[:, :, i * width : (i + 1) * width])
             return raw
 
-        def load_rows(src, t, name, pieces=1):
-            rows = keep.tile([P, S], F32, name=name)
-            for i in range(pieces):
-                cols = slice(i * S // pieces, (i + 1) * S // pieces)
-                nc.sync.dma_start(rows[:, cols], src.rearrange("(p t) s -> p t s", t=PACK)[:, t, cols])
-            return rows
+        def load_rows(rows, src, t, cols):
+            nc.sync.dma_start(rows[:, cols], src.rearrange("(p t) s -> p t s", t=PACK)[:, t, cols])
 
+        off_sb = [keep.tile([P, S], F32, name="off%d" % t) for t in range(PACK)]
         nc.sync.dma_start(offs_sb[:], offs)
-        w1_raw = [load_weight_half(w1, 0, "w1_raw0")]
+        nc.sync.dma_start(qry_sb[:], qry)
         for q in range(4):
             nc.sync.dma_start(
                 table_scales[32 * q : 32 * q + 4, :].bitcast(I32), x_scales[0][4 * q : 4 * q + 4, :].bitcast(I32)
             )
-        w1_raw.append(load_weight_half(w1, 1, "w1_raw1"))
         nc.sync.dma_start(table_words[:], x_words[0].rearrange("p c r -> p (c r)").bitcast(I32))
-        w2_raw = [load_weight_half(w2, h, "w2_raw%d" % h) for h in range(2)]
-        off_sb = [load_rows(off, 0, "off0", pieces=2)]
-        off_sb.extend(load_rows(off, t, "off%d" % t) for t in range(1, PACK))
-        sg_sb = [load_rows(sg, t, "sg%d" % t) for t in range(PACK)]
+        w1_raw = [load_weight_piece(w1, i, W1_PIECES, "w1_raw") for i in range(W1_PIECES)]
+        w2_raw = [load_weight_piece(w2, 0, 2, "w2_raw")]
+        load_rows(off_sb[0], off, 0, slice(0, HALF))
+        w2_raw.append(load_weight_piece(w2, 1, 2, "w2_raw"))
+        load_rows(off_sb[0], off, 0, slice(HALF, S))
+        for t in range(1, PACK):
+            load_rows(off_sb[t], off, t, slice(0, S))
+        sg_sb = [keep.tile([P, S], F32, name="sg%d" % t) for t in range(PACK)]
+        for t in range(PACK):
+            load_rows(sg_sb[t], sg, t, slice(0, S))
         w3_raw = keep.tile([P, PACK, N], F32, name="w3_raw")
         nc.sync.dma_start(w3_raw[:], w3.rearrange("(p j) n -> p j n", j=PACK))
         unit_sb = keep.tile([P, PACK], F32, name="unit_sb")
         nc.sync.dma_start(unit_sb[:], unit.rearrange("(p t) o -> p (t o)", t=PACK))
-        nc.sync.dma_start(qry_sb[:], qry)
 
         ident = keep.tile([P, P], F32, name="ident")
         make_identity(nc, ident[:])
 
-        def round_weight(raw_halves, name):
+        def round_weight(raw, name, factor):
             grouped = keep.tile([P, PACK, P, PACK], BF16, name=name, align_bytes=64)
-            for h in range(2):
-                nc.scalar.activation(
-                    out=grouped[:, :, h * (P // 2) : (h + 1) * (P // 2), :].rearrange("p t m j -> p m t j"),
-                    in_=raw_halves[h][:].rearrange("p j (m t) -> p m t j", t=PACK),
-                    func=ACT.Copy,
-                )
+            width = P // len(raw)
+            for i in range(len(raw)):
+                dst = grouped[:, :, i * width : (i + 1) * width, :].rearrange("p t m j -> p m t j")
+                src = raw[i][:].rearrange("p j (m t) -> p m t j", t=PACK)
+                nc.scalar.activation(out=dst, in_=src, func=ACT.Copy, scale=factor)
             return grouped[:].rearrange("p t m j -> p (t m j)")
 
         def quantize(grouped, name):
@@ -93,204 +95,189 @@ def tile_picked_yimlsq_nrm_p_kernel(
             nc.vector.quantize_mx(out=codes[:].bitcast(FP8X4), scales=scales[:], in_=grouped)
             return codes, scales
 
-        picked_scales = keep.tile([P, S], U8, name="picked_scales")
+        picked_scales = keep.tile([P, S], U8, name="picked_scales", align_bytes=64)
         nc.vector.tensor_copy(picked_scales[:], table_scales[:].indirect(offs_sb[:]))
-        dealt_scales = keep.tile([P, S], U8, name="dealt_scales", align_bytes=64)
-        nc.vector.tensor_copy(
-            dealt_scales[:].rearrange("p (h d v) -> p h d v", h=2, d=D),
-            picked_scales[:].rearrange("p (h v d) -> p h d v", h=2, d=D),
-        )
-        x_scale = [dealt_scales[:, vh * HALF : (vh + 1) * HALF] for vh in range(2)]
-        w1_codes, w1_scales = quantize(round_weight(w1_raw, "w1_grouped"), "w1")
-        x_code = []
+        picked_words = keep.tile([P, S], U32, name="picked_words", align_bytes=64)
         for vh in range(2):
-            words = keep.tile([P, HALF], U32, name="picked_words%d" % vh, align_bytes=64)
             cols = HALF // LIST_COLS
             nc.vector.tensor_copy(
-                words[:].rearrange("p (d v) -> p v d", d=D),
+                picked_words[:, vh * HALF : (vh + 1) * HALF],
                 table_words[:].bitcast(U32).indirect(offs_sb[:, vh * cols : (vh + 1) * cols]),
             )
-            x_code.append(words)
-
-        chunks = [(t, vh) for t in range(PACK) for vh in range(2)]
-        last = len(chunks) - 1
+        w1_codes, w1_scales = quantize(round_weight(w1_raw, "w1_grouped", -0.5), "w1")
+        dealt_scales = keep.tile([P, S], U8, name="dealt_scales", tag="w1_raw1", align_bytes=64)
+        nc.vector.tensor_copy(
+            dealt_scales[:].rearrange("p (d v) -> p d v", d=D), picked_scales[:].rearrange("p (v d) -> p d v", d=D)
+        )
+        dealt_words = keep.tile([P, S], U32, name="dealt_words", tag="w1_grouped", align_bytes=64)
+        nc.vector.tensor_copy(
+            dealt_words[:].rearrange("p (d c i) -> p c d i", d=D, i=4),
+            picked_words[:].rearrange("p (c i d) -> p c d i", d=D, i=4),
+        )
 
         def feature_cols(t):
             return slice(t * P, (t + 1) * P)
 
-        def paired(tile_ap):
-            return tile_ap.rearrange("p (a v b) -> p a v b", a=2, b=2)
+        def paired(rows, cells):
+            return rows[:].rearrange("p (a v b) -> p a v b", a=2, b=2)[:, :, cells, :]
 
-        def given(rows, vh):
-            return rows[:, vh * HALF : (vh + 1) * HALF].rearrange("p (v a b) -> p a v b", a=2, b=2)
+        def listed(rows, cells):
+            return rows[:].rearrange("p (v a b) -> p a v b", a=2, b=2)[:, :, cells, :]
 
-        def group_sums(bank, slot, values):
-            for d in range(D):
-                first = (d // 2) * 2 * VH + d % 2
-                nc.tensor.matmul(
-                    bank[:, slot * P : (slot + 1) * P],
-                    lhsT=values[:, first : first + 2 * VH - d % 2 : 2],
-                    rhs=ident[:],
-                    is_transpose=True,
-                    start=(d == 0),
-                    stop=(d == D - 1),
-                )
+        def group_sums(bank, first_col, values, cells):
+            for v0 in range(cells.start, cells.stop, P):
+                for d in range(D):
+                    nc.tensor.matmul(
+                        bank[:, first_col + v0 : first_col + v0 + P],
+                        lhsT=paired(values, slice(v0, v0 + P))[:, d // 2, :, d % 2],
+                        rhs=ident[:],
+                        is_transpose=True,
+                        start=(d == 0),
+                        stop=(d == D - 1),
+                    )
 
-        fx = [keep.tile([P, HALF], F32, name="fx%d" % c) for c in range(len(chunks))]
-        we0 = [keep.tile([P, HALF], F32, name="we0_%d" % c) for c in range(len(chunks))]
+        halves = [slice(0, VH), slice(VH, V)]
+        whole = slice(0, V)
+        chunks = [(t, vh) for t in range(PACK) for vh in range(2)]
+        last = len(chunks) - 1
+
+        fx = [keep.tile([P, S], F32, name="fx%d" % t, align_bytes=64) for t in range(PACK)]
+        we0 = [keep.tile([P, S], F32, name="we0_%d" % t) for t in range(PACK)]
+        wf = [keep.tile([P, S], F32, name="wf%d" % t) for t in range(PACK)]
         tanh_nm = [keep.tile([P, 2 * V], F32, name="tanh_nm%d" % i) for i in range(2)]
-        last_square = keep.tile([P, HALF], F32, name="last_square")
-        weight_sums0 = {}
-        value_sums0 = {}
+        work = [keep.tile([P, S], F32, name="work%d" % t) for t in range(PACK)]
+        sums0 = {}
 
         def offsets_of(c):
             t, vh = chunks[c]
-            tag = "bank%d" % (c % 6)
-            py = psum.tile([P, HALF], F32, name="py%d" % c, tag=tag)
+            py = psum.tile([P, HALF], F32, name="py%d" % c, tag="bank%d" % (c % 4))
             nc.tensor.matmul_mx(
                 py[:],
                 lhsT=w1_codes[:, feature_cols(t)].bitcast(FP8X4),
                 lhsT_scale=w1_scales[:, feature_cols(t)],
-                rhs=x_code[vh][:].bitcast(FP8X4),
-                rhs_scale=x_scale[vh],
+                rhs=picked_words[:, vh * HALF : (vh + 1) * HALF].bitcast(FP8X4),
+                rhs_scale=picked_scales[:, vh * HALF : (vh + 1) * HALF],
                 start=True,
                 stop=True,
             )
-            py_view = py[:].rearrange("p (a b v) -> p a v b", a=2, b=2)
-            for a in range(2):
-                nc.vector.scalar_tensor_tensor(
-                    out=paired(fx[c][:])[:, a],
-                    in0=py_view[:, a],
-                    scalar=-0.5,
-                    in1=given(off_sb[t], vh)[:, a],
-                    op0=ALU.mult,
-                    op1=ALU.add,
-                )
+            nc.vector.tensor_tensor(
+                out=paired(fx[t], halves[vh]),
+                in0=listed(py, slice(0, VH)),
+                in1=listed(off_sb[t], halves[vh]),
+                op=ALU.add,
+            )
 
-        def first_weights(c):
-            if c == last:
-                square = last_square
-            else:
-                square = ring.tile([P, HALF], F32, name="square", tag="square")
-            nc.scalar.activation(out=square[:], in_=fx[c][:], func=ACT.Square, scale=0.6)
-            nc.scalar.activation(out=we0[c][:], in_=square[:], func=ACT.Exp, scale=-1.0)
+        def first_weights(t, cells):
+            nc.scalar.activation(out=paired(work[t], cells), in_=paired(fx[t], cells), func=ACT.Square, scale=0.6)
+            nc.scalar.activation(out=paired(we0[t], cells), in_=paired(work[t], cells), func=ACT.Exp, scale=-1.0)
 
-        wf = [keep.tile([P, HALF], F32, name="wf%d" % c) for c in range(len(chunks))]
+        def weighted_offsets(t, cells):
+            nc.vector.tensor_tensor(
+                out=paired(wf[t], cells), in0=paired(we0[t], cells), in1=paired(fx[t], cells), op=ALU.mult
+            )
 
-        def weighted_offsets(c):
-            nc.vector.tensor_tensor(out=wf[c][:], in0=we0[c][:], in1=fx[c][:], op=ALU.mult)
-
-        def first_sums(c):
-            if c % 4 == 0:
-                weight_sums0[c // 4] = psum.tile([P, 4 * P], F32, name="s0", tag=WEIGHT_BANKS[c // 4])
-                value_sums0[c // 4] = psum.tile([P, 4 * P], F32, name="n0", tag=VALUE_BANKS[c // 4])
-            group_sums(weight_sums0[c // 4], c % 4, we0[c])
-            group_sums(value_sums0[c // 4], c % 4, wf[c])
+        def first_sums(t):
+            sums0[t] = psum.tile([P, 2 * V], F32, name="sums0", tag="bank%d" % ((6 + t) % 8))
+            group_sums(sums0[t], 0, we0[t], whole)
+            group_sums(sums0[t], V, wf[t], whole)
 
         def normals(w2_codes, w2_scales):
             for i in range(2):
-                bank = psum.tile([P, 2 * V], F32, name="normal%d" % i, tag="bank%d" % (6 + i))
-                for s in range(4):
-                    t, vh = 2 * i + s // 2, s % 2
+                bank = psum.tile([P, 2 * V], F32, name="normal%d" % i, tag="bank%d" % (4 + i))
+                for t in (2 * i, 2 * i + 1):
                     for d in range(D):
                         nc.tensor.matmul_mx(
-                            bank[:, s * VH : (s + 1) * VH],
+                            bank[:, (t % 2) * V : (t % 2 + 1) * V],
                             lhsT=w2_codes[:, feature_cols(t)].bitcast(FP8X4),
                             lhsT_scale=w2_scales[:, feature_cols(t)],
-                            rhs=x_code[vh][:, d * VH : (d + 1) * VH].bitcast(FP8X4),
-                            rhs_scale=x_scale[vh][:, d * VH : (d + 1) * VH],
+                            rhs=dealt_words[:, d * V : (d + 1) * V].bitcast(FP8X4),
+                            rhs_scale=dealt_scales[:, d * V : (d + 1) * V],
                             start=(d == 0),
                             stop=(d == D - 1),
                         )
                 nc.scalar.activation(out=tanh_nm[i][:], in_=bank[:], func=ACT.Tanh, scale=1.0 / D)
 
-        w2_grouped = round_weight(w2_raw, "w2_grouped")
-        for step in range(len(chunks) + 1):
-            if step == 6:
-                normals(*quantize(w2_grouped, "w2"))
-            if step < len(chunks):
-                offsets_of(step)
-            if step >= 1:
-                first_weights(step - 1)
         for c in range(len(chunks)):
-            weighted_offsets(c)
-        for c in range(4):
-            first_sums(c)
+            offsets_of(c)
+        w2_grouped = round_weight(w2_raw, "w2_grouped", 1.0)
+        w2_codes, w2_scales = quantize(w2_grouped, "w2")
+        for t, cells in [(0, halves[0]), (0, halves[1]), (1, whole), (2, whole), (3, halves[0]), (3, halves[1])]:
+            if t == 3 and cells.start == 0:
+                normals(w2_codes, w2_scales)
+            first_weights(t, cells)
+        for t, cells in [(t, whole) for t in range(PACK)]:
+            weighted_offsets(t, cells)
+        for t in range(PACK):
+            first_sums(t)
 
-        def group_mean(weight_sums, value_sums, inverse, turned):
+        def group_mean(weight_sums, value_sums, squared, inverse, turned):
             width = inverse.shape[1]
-            squared = ring.tile([P, width], F32, name="squared", tag="squared")
-            nc.scalar.activation(out=squared[:], in_=weight_sums, func=ACT.Square, bias=0.1)
-            nc.scalar.activation(out=inverse, in_=squared[:], func=ACT.Abs_reciprocal_sqrt)
+            nc.scalar.activation(out=squared, in_=weight_sums, func=ACT.Square, bias=0.1)
+            nc.scalar.activation(out=inverse, in_=squared, func=ACT.Abs_reciprocal_sqrt)
             mean = ring.tile([P, width], F32, name="mean", tag="mean")
             nc.vector.tensor_tensor(out=mean[:], in0=value_sums, in1=inverse, op=ALU.mult)
             for s in range(width // P):
                 nc.tensor.transpose(turned[:, s * P : (s + 1) * P], mean[:, s * P : (s + 1) * P], ident[:])
 
-        scaled = [keep.tile([P, HALF], F32, name="scaled%d" % c) for c in range(len(chunks))]
-        cells = [keep.tile([P, V], F32, name="cells%d" % t) for t in range(PACK)]
+        scaled = [keep.tile([P, S], F32, name="scaled%d" % t) for t in range(PACK)]
+        cell_values = [keep.tile([P, V], F32, name="cells%d" % t) for t in range(PACK)]
         m0 = {}
         m1 = {}
-        size = {}
-        inverse_size = {}
         weight_sums1 = {}
         value_sums1 = {}
         picked_hid = keep.tile([P, PACK, U], BF16, name="picked_hid")
 
-        def first_mean(i):
-            m0[i] = psum.tile([P, 4 * VH], F32, name="m0_%d" % i, tag="bank%d" % (4 + i))
-            if i == 0:
-                inverse = last_square
-            else:
-                inverse = ring.tile([P, HALF], F32, name="inverse", tag="inverse")
-            group_mean(weight_sums0[i][:], value_sums0[i][:], inverse[:], m0[i])
+        def first_mean(t):
+            m0[t] = psum.tile([P, V], F32, name="m0_%d" % t, tag="bank%d" % (2 + t))
+            first = (t % 2) * HALF + V
+            squared = ring.tile([P, V], F32, name="squared", tag="squared")
+            group_mean(sums0[t][:, 0:V], sums0[t][:, V : 2 * V], squared[:], work[PACK - 1][:, first : first + V], m0[t])
 
-        def scale_weights(c):
-            t, vh = chunks[c]
+        def scale_weights(t):
             nc.vector.tensor_tensor(
-                out=paired(scaled[c][:]), in0=paired(we0[c][:]), in1=given(sg_sb[t], vh), op=ALU.mult
+                out=paired(scaled[t], whole), in0=paired(we0[t], whole), in1=listed(sg_sb[t], whole), op=ALU.mult
             )
 
-        def residual(c):
-            res = ring.tile([P, HALF], F32, name="res", tag="res")
-            mean = m0[c // 4][:, (c % 4) * VH : (c % 4 + 1) * VH]
-            spread = mean.unsqueeze(1).unsqueeze(3).to_broadcast([P, 2, VH, 2])
-            nc.vector.tensor_tensor(out=paired(res[:]), in0=paired(fx[c][:]), in1=spread, op=ALU.subtract)
-            size[c] = ring.tile([P, HALF], F32, name="size", tag="size")
-            nc.scalar.activation(out=size[c][:], in_=res[:], func=ACT.Abs)
+        def residual(t, cells):
+            res = paired(work[t], cells)
+            spread = m0[t][:, cells].unsqueeze(1).unsqueeze(3).to_broadcast([P, 2, cells.stop - cells.start, 2])
+            nc.vector.tensor_tensor(out=res, in0=paired(fx[t], cells), in1=spread, op=ALU.subtract)
+            nc.scalar.activation(out=res, in_=res, func=ACT.Abs)
 
-        def denominators(c):
-            t, vh = chunks[c]
-            denom = ring.tile([P, HALF], F32, name="denom", tag="denom")
-            nc.vector.tensor_tensor(out=paired(denom[:]), in0=paired(size[c][:]), in1=given(sg_sb[t], vh), op=ALU.add)
-            denom_sq = ring.tile([P, HALF], F32, name="denom_sq", tag="denom_sq")
-            nc.scalar.activation(out=denom_sq[:], in_=denom[:], func=ACT.Square)
-            inverse_size[c] = ring.tile([P, HALF], F32, name="inverse_size", tag="inverse_size")
-            nc.scalar.activation(out=inverse_size[c][:], in_=denom_sq[:], func=ACT.Abs_reciprocal_sqrt)
+        def denominators(t, cells):
+            denom = paired(work[t], cells)
+            nc.vector.tensor_tensor(out=denom, in0=denom, in1=listed(sg_sb[t], cells), op=ALU.add)
+            nc.scalar.activation(out=denom, in_=denom, func=ACT.Square)
+            nc.scalar.activation(out=denom, in_=denom, func=ACT.Abs_reciprocal_sqrt)
 
-        def second_sums(c):
-            t, vh = chunks[c]
-            if vh == 0:
-                weight_sums1[t] = psum.tile([P, V], F32, name="s1_%d" % t, tag=WEIGHT_BANKS[t % 2])
-                value_sums1[t] = psum.tile([P, V], F32, name="n1_%d" % t, tag=VALUE_BANKS[t % 2])
-            we1 = ring.tile([P, HALF], F32, name="we1", tag="we1")
-            nc.vector.tensor_tensor(out=we1[:], in0=scaled[c][:], in1=inverse_size[c][:], op=ALU.mult)
-            wf1 = ring.tile([P, HALF], F32, name="wf1", tag="wf")
-            nc.vector.tensor_tensor(out=wf1[:], in0=we1[:], in1=fx[c][:], op=ALU.mult)
-            group_sums(weight_sums1[t], vh, we1)
-            group_sums(value_sums1[t], vh, wf1)
+        def second_sums(t, cells):
+            if cells.start == 0:
+                weight_sums1[t] = psum.tile([P, V], F32, name="s1_%d" % t, tag="bank%d" % ((6 + 2 * t) % 4 + 4 * (1 - t % 2)))
+                value_sums1[t] = psum.tile([P, V], F32, name="n1_%d" % t, tag="bank%d" % ((7 + 2 * t) % 4 + 4 * (1 - t % 2)))
+            we1 = paired(work[t], cells)
+            nc.vector.tensor_tensor(out=we1, in0=paired(scaled[t], cells), in1=we1, op=ALU.mult)
+            nc.vector.tensor_tensor(out=paired(wf[t], cells), in0=we1, in1=paired(fx[t], cells), op=ALU.mult)
+            group_sums(weight_sums1[t], 0, work[t], cells)
+            group_sums(value_sums1[t], 0, wf[t], cells)
 
-        def hidden(t, first, count):
-            if first == 0:
-                m1[t] = psum.tile([P, V], F32, name="m1_%d" % t, tag="bank%d" % (t % 2))
-            cols = slice(first, first + count)
-            inverse = ring.tile([P, count], F32, name="inverse", tag="inverse")
-            group_mean(weight_sums1[t][:, cols], value_sums1[t][:, cols], inverse[:], m1[t][:, cols])
+        def hidden(t, cells):
+            if t < PACK - 1:
+                if cells.stop < V:
+                    return
+                cells = whole
+            if cells.start == 0:
+                m1[t] = psum.tile([P, V], F32, name="m1_%d" % t, tag="bank%d" % (2 + t))
+            inverse = ring.tile([P, cells.stop - cells.start], F32, name="inverse", tag="inverse")
+            if t == PACK - 1:
+                squared = picked_hid[:, PACK - 2, :].bitcast(F32)[:, cells]
+            else:
+                squared = ring.tile([P, V], F32, name="squared", tag="squared")[:]
+            group_mean(weight_sums1[t][:, cells], value_sums1[t][:, cells], squared, inverse[:], m1[t][:, cells])
             nc.vector.scalar_tensor_tensor(
-                out=cells[t][:, cols],
-                in0=m1[t][:, cols],
+                out=cell_values[t][:, cells],
+                in0=m1[t][:, cells],
                 scalar=unit_sb[:, t : t + 1],
-                in1=tanh_nm[t // 2][:, (t % 2) * V + first : (t % 2) * V + first + count],
+                in1=tanh_nm[t // 2][:, (t % 2) * V + cells.start : (t % 2) * V + cells.stop],
                 op0=ALU.mult,
                 op1=ALU.mult,
             )
@@ -298,34 +285,32 @@ def tile_picked_yimlsq_nrm_p_kernel(
         def look_up(t, s, on_vector):
             cols = QUERY_SLICE // LIST_COLS
             picked = picked_hid[:, t, s * QUERY_SLICE : (s + 1) * QUERY_SLICE]
-            window = cells[t][:].indirect(qry_sb[:, s * cols : (s + 1) * cols])
+            window = cell_values[t][:].indirect(qry_sb[:, s * cols : (s + 1) * cols])
             if on_vector:
                 nc.vector.tensor_copy(picked, window)
             else:
                 nc.scalar.activation(out=picked, in_=window, func=ACT.Copy)
 
-        first_mean(0)
-        for c in range(4, len(chunks)):
-            first_sums(c)
-        first_mean(1)
-        for step in range(len(chunks) + 3):
-            if step < len(chunks):
-                residual(step)
-            if 0 <= step - 1 < len(chunks):
-                denominators(step - 1)
-                scale_weights(step - 1)
-            if step == last + 2:
-                hidden(PACK - 1, 0, VH)
-            if 0 <= step - 2 < len(chunks):
-                second_sums(step - 2)
-            if step in (4, 6, 8):
-                hidden(step // 2 - 2, 0, V)
-        hidden(PACK - 1, VH, VH)
+        steps = [(t, whole) for t in range(PACK - 1)] + [(PACK - 1, halves[0]), (PACK - 1, halves[1])]
         for t in range(PACK):
+            first_mean(t)
+        for step in range(len(steps) + 4 + 1):
+            if step < len(steps):
+                residual(*steps[step])
+            if 0 <= step - 1 < len(steps):
+                denominators(*steps[step - 1])
+            if step == 0:
+                for t in range(PACK):
+                    scale_weights(t)
+            if 0 <= step - 4 - 1 < len(steps):
+                hidden(*steps[step - 4 - 1])
+            if 0 <= step - 4 < len(steps):
+                second_sums(*steps[step - 4])
+        for t in range(0, PACK):
             for s in range(U // QUERY_SLICE):
                 look_up(t, s, t == PACK - 1 and s % 2 == 0)
 
-        w3_grouped = keep.tile([P, N, PACK], BF16, name="w3_grouped", align_bytes=64)
+        w3_grouped = keep.tile([P, N, PACK], BF16, name="w3_grouped", tag="fx0", align_bytes=64)
         nc.scalar.activation(out=w3_grouped[:], in_=w3_raw[:].rearrange("p j n -> p n j"), func=ACT.Copy)
         w3_codes, w3_scales = quantize(w3_grouped[:].rearrange("p n j -> p (n j)"), "w3")
         for h in range(2):
@@ -336,7 +321,7 @@ def tile_picked_yimlsq_nrm_p_kernel(
                 picked_hid[:, :, queries].rearrange("p t (c i) -> p c t i", i=4),
             )
             hid_codes, hid_scales = quantize(hid[:].rearrange("p r t -> p (r t)"), "hid%d" % h)
-            patches = psum.tile([P, U // 2], F32, name="patches%d" % h, tag="bank%d" % (4 + h))
+            patches = psum.tile([P, U // 2], F32, name="patches%d" % h, tag="bank%d" % (2 + h))
             nc.tensor.matmul_mx(
                 patches[:],
                 lhsT=w3_codes[:].bitcast(FP8X4),

@@ -124,12 +124,21 @@ def tile_picked_yimlsq_nrm_p_kernel(
         def listed(rows, cells):
             return rows[:].rearrange("p (v a b) -> p a v b", a=2, b=2)[:, :, cells, :]
 
+        def paired_by_point(rows, cells):
+            return rows[:].rearrange("p (a v b) -> p a b v", a=2, b=2)[:, :, :, cells]
+
+        def by_point(rows, cells):
+            return rows[:].rearrange("p (a b v) -> p a b v", a=2, b=2)[:, :, :, cells]
+
+        def by_point_paired(rows, cells):
+            return rows[:].rearrange("p (a b v) -> p a v b", a=2, b=2)[:, :, cells, :]
+
         def group_sums(bank, first_col, values, cells):
             for v0 in range(cells.start, cells.stop, P):
                 for d in range(D):
                     nc.tensor.matmul(
                         bank[:, first_col + v0 : first_col + v0 + P],
-                        lhsT=paired(values, slice(v0, v0 + P))[:, d // 2, :, d % 2],
+                        lhsT=values[:, d * V + v0 : d * V + v0 + P],
                         rhs=ident[:],
                         is_transpose=True,
                         start=(d == 0),
@@ -168,16 +177,17 @@ def tile_picked_yimlsq_nrm_p_kernel(
             )
 
         def first_weights(t, cells):
-            nc.scalar.activation(out=paired(work[t], cells), in_=paired(fx[t], cells), func=ACT.Square, scale=0.6)
-            nc.scalar.activation(out=paired(we0[t], cells), in_=paired(work[t], cells), func=ACT.Exp, scale=-1.0)
+            square = by_point(work[t], cells)
+            nc.scalar.activation(out=square, in_=paired_by_point(fx[t], cells), func=ACT.Square, scale=0.6)
+            nc.scalar.activation(out=by_point(we0[t], cells), in_=square, func=ACT.Exp, scale=-1.0)
 
         def weighted_offsets(t, cells):
             nc.vector.tensor_tensor(
-                out=paired(wf[t], cells), in0=paired(we0[t], cells), in1=paired(fx[t], cells), op=ALU.mult
+                out=by_point(wf[t], cells), in0=by_point(we0[t], cells), in1=paired_by_point(fx[t], cells), op=ALU.mult
             )
 
         def first_sums(t):
-            sums0[t] = psum.tile([P, 2 * V], F32, name="sums0", tag="bank%d" % ((6 + t) % 8))
+            sums0[t] = psum.tile([P, 2 * V], F32, name="sums0", tag="bank%d" % (6, 7, 0, 1)[t])
             group_sums(sums0[t], 0, we0[t], whole)
             group_sums(sums0[t], V, wf[t], whole)
 
@@ -207,7 +217,7 @@ def tile_picked_yimlsq_nrm_p_kernel(
             first_weights(t, cells)
         for t, cells in [(t, whole) for t in range(PACK)]:
             weighted_offsets(t, cells)
-        for t in range(PACK):
+        for t in range(3):
             first_sums(t)
 
         def group_mean(weight_sums, value_sums, squared, inverse, turned):
@@ -220,7 +230,6 @@ def tile_picked_yimlsq_nrm_p_kernel(
                 nc.tensor.transpose(turned[:, s * P : (s + 1) * P], mean[:, s * P : (s + 1) * P], ident[:])
 
         scaled = [keep.tile([P, S], F32, name="scaled%d" % t) for t in range(PACK)]
-        cell_values = [keep.tile([P, V], F32, name="cells%d" % t) for t in range(PACK)]
         m0 = {}
         m1 = {}
         weight_sums1 = {}
@@ -229,13 +238,13 @@ def tile_picked_yimlsq_nrm_p_kernel(
 
         def first_mean(t):
             m0[t] = psum.tile([P, V], F32, name="m0_%d" % t, tag="bank%d" % (2 + t))
-            first = (t % 2) * HALF + V
+            first = t * V
             squared = ring.tile([P, V], F32, name="squared", tag="squared")
             group_mean(sums0[t][:, 0:V], sums0[t][:, V : 2 * V], squared[:], work[PACK - 1][:, first : first + V], m0[t])
 
         def scale_weights(t):
             nc.vector.tensor_tensor(
-                out=paired(scaled[t], whole), in0=paired(we0[t], whole), in1=listed(sg_sb[t], whole), op=ALU.mult
+                out=paired(scaled[t], whole), in0=by_point_paired(we0[t], whole), in1=listed(sg_sb[t], whole), op=ALU.mult
             )
 
         def residual(t, cells):
@@ -247,17 +256,18 @@ def tile_picked_yimlsq_nrm_p_kernel(
         def denominators(t, cells):
             denom = paired(work[t], cells)
             nc.vector.tensor_tensor(out=denom, in0=denom, in1=listed(sg_sb[t], cells), op=ALU.add)
-            nc.scalar.activation(out=denom, in_=denom, func=ACT.Square)
-            nc.scalar.activation(out=denom, in_=denom, func=ACT.Abs_reciprocal_sqrt)
+            inverse = by_point(we0[t], cells)
+            nc.scalar.activation(out=inverse, in_=paired_by_point(work[t], cells), func=ACT.Square)
+            nc.scalar.activation(out=inverse, in_=inverse, func=ACT.Abs_reciprocal_sqrt)
 
         def second_sums(t, cells):
             if cells.start == 0:
-                weight_sums1[t] = psum.tile([P, V], F32, name="s1_%d" % t, tag="bank%d" % ((6 + 2 * t) % 4 + 4 * (1 - t % 2)))
-                value_sums1[t] = psum.tile([P, V], F32, name="n1_%d" % t, tag="bank%d" % ((7 + 2 * t) % 4 + 4 * (1 - t % 2)))
-            we1 = paired(work[t], cells)
-            nc.vector.tensor_tensor(out=we1, in0=paired(scaled[t], cells), in1=we1, op=ALU.mult)
-            nc.vector.tensor_tensor(out=paired(wf[t], cells), in0=we1, in1=paired(fx[t], cells), op=ALU.mult)
-            group_sums(weight_sums1[t], 0, work[t], cells)
+                weight_sums1[t] = psum.tile([P, V], F32, name="s1_%d" % t, tag="bank%d" % (6 * (t % 2)))
+                value_sums1[t] = psum.tile([P, V], F32, name="n1_%d" % t, tag="bank%d" % (6 * (t % 2) + 1))
+            we1 = by_point(we0[t], cells)
+            nc.vector.tensor_tensor(out=we1, in0=paired_by_point(scaled[t], cells), in1=we1, op=ALU.mult)
+            nc.vector.tensor_tensor(out=by_point(wf[t], cells), in0=we1, in1=paired_by_point(fx[t], cells), op=ALU.mult)
+            group_sums(weight_sums1[t], 0, we0[t], cells)
             group_sums(value_sums1[t], 0, wf[t], cells)
 
         def hidden(t, cells):
@@ -274,7 +284,7 @@ def tile_picked_yimlsq_nrm_p_kernel(
                 squared = ring.tile([P, V], F32, name="squared", tag="squared")[:]
             group_mean(weight_sums1[t][:, cells], value_sums1[t][:, cells], squared, inverse[:], m1[t][:, cells])
             nc.vector.scalar_tensor_tensor(
-                out=cell_values[t][:, cells],
+                out=scaled[t][:, cells],
                 in0=m1[t][:, cells],
                 scalar=unit_sb[:, t : t + 1],
                 in1=tanh_nm[t // 2][:, (t % 2) * V + cells.start : (t % 2) * V + cells.stop],
@@ -282,33 +292,33 @@ def tile_picked_yimlsq_nrm_p_kernel(
                 op1=ALU.mult,
             )
 
-        def look_up(t, s, on_vector):
-            cols = QUERY_SLICE // LIST_COLS
-            picked = picked_hid[:, t, s * QUERY_SLICE : (s + 1) * QUERY_SLICE]
-            window = cell_values[t][:].indirect(qry_sb[:, s * cols : (s + 1) * cols])
+        def look_up(t, queries, on_vector):
+            window = scaled[t][:].indirect(qry_sb[:, queries.start // LIST_COLS : queries.stop // LIST_COLS])
             if on_vector:
-                nc.vector.tensor_copy(picked, window)
+                nc.vector.tensor_copy(picked_hid[:, t, queries], window)
             else:
-                nc.scalar.activation(out=picked, in_=window, func=ACT.Copy)
+                nc.scalar.activation(out=picked_hid[:, t, queries], in_=window, func=ACT.Copy)
 
         steps = [(t, whole) for t in range(PACK - 1)] + [(PACK - 1, halves[0]), (PACK - 1, halves[1])]
-        for t in range(PACK):
+        for t in range(2):
             first_mean(t)
-        for step in range(len(steps) + 4 + 1):
+        first_sums(PACK - 1)
+        for step in range(len(steps) + 2 + 1):
             if step < len(steps):
+                if steps[step][0] not in m0:
+                    first_mean(steps[step][0])
                 residual(*steps[step])
-            if 0 <= step - 1 < len(steps):
-                denominators(*steps[step - 1])
             if step == 0:
                 for t in range(PACK):
                     scale_weights(t)
-            if 0 <= step - 4 - 1 < len(steps):
-                hidden(*steps[step - 4 - 1])
-            if 0 <= step - 4 < len(steps):
-                second_sums(*steps[step - 4])
-        for t in range(0, PACK):
-            for s in range(U // QUERY_SLICE):
-                look_up(t, s, t == PACK - 1 and s % 2 == 0)
+            if 0 <= step - 1 < len(steps):
+                denominators(*steps[step - 1])
+            if 0 <= step - 2 - 1 < len(steps):
+                hidden(*steps[step - 2 - 1])
+            if 0 <= step - 2 < len(steps):
+                second_sums(*steps[step - 2])
+        for t, first, count, on_vector in [(t, 256 * h, 256, False) for t in range(3) for h in range(2)] + [(3, 0, 128, True), (3, 128, 128, False), (3, 256, 256, False)]:
+            look_up(t, slice(first, first + count), on_vector)
 
         w3_grouped = keep.tile([P, N, PACK], BF16, name="w3_grouped", tag="fx0", align_bytes=64)
         nc.scalar.activation(out=w3_grouped[:], in_=w3_raw[:].rearrange("p j n -> p n j"), func=ACT.Copy)

@@ -14,6 +14,7 @@ U8 = mybir.dt.uint8
 FP8X4 = mybir.dt.float8_e4m3fn_x4
 ACT = mybir.ActivationFunctionType
 ALU = mybir.AluOpType
+AXIS = mybir.AxisListType
 
 P = 128
 PACK = 4
@@ -22,7 +23,7 @@ HALF = S // 2
 VH = V // 2
 QUERY_SLICE = 128
 LIST_COLS = 16
-W1_PIECES = 4
+W1_PIECES = 2
 WEIGHT_BANKS = ("bank7", "bank2")
 VALUE_BANKS = ("bank6", "bank3")
 
@@ -62,12 +63,14 @@ def tile_picked_yimlsq_nrm_p_kernel(
             )
         nc.sync.dma_start(table_words[:], x_words[0].rearrange("p c r -> p (c r)").bitcast(I32))
         w1_raw = [load_weight_piece(w1, i, W1_PIECES, "w1_raw") for i in range(W1_PIECES)]
-        w2_raw = [load_weight_piece(w2, 0, 2, "w2_raw")]
-        load_rows(off_sb[0], off, 0, slice(0, HALF))
-        w2_raw.append(load_weight_piece(w2, 1, 2, "w2_raw"))
-        load_rows(off_sb[0], off, 0, slice(HALF, S))
-        for t in range(1, PACK):
-            load_rows(off_sb[t], off, t, slice(0, S))
+        w2_raw = []
+        for what, i in [("w2",0),("half",0),("w2",1),("half",1),("off",1),("off",2),("off",3)]:
+            if what == "w2":
+                w2_raw.append(load_weight_piece(w2, i, 2, "w2_raw"))
+            elif what == "half":
+                load_rows(off_sb[0], off, 0, slice(i * HALF, (i + 1) * HALF))
+            else:
+                load_rows(off_sb[i], off, i, slice(0, S))
         sg_sb = [keep.tile([P, S], F32, name="sg%d" % t) for t in range(PACK)]
         for t in range(PACK):
             load_rows(sg_sb[t], sg, t, slice(0, S))
@@ -105,11 +108,11 @@ def tile_picked_yimlsq_nrm_p_kernel(
                 table_words[:].bitcast(U32).indirect(offs_sb[:, vh * cols : (vh + 1) * cols]),
             )
         w1_codes, w1_scales = quantize(round_weight(w1_raw, "w1_grouped", -0.5), "w1")
-        dealt_scales = keep.tile([P, S], U8, name="dealt_scales", tag="w1_raw1", align_bytes=64)
+        dealt_scales = keep.tile([P, S], U8, name="dealt_scales", align_bytes=64)
         nc.vector.tensor_copy(
             dealt_scales[:].rearrange("p (d v) -> p d v", d=D), picked_scales[:].rearrange("p (v d) -> p d v", d=D)
         )
-        dealt_words = keep.tile([P, S], U32, name="dealt_words", tag="w1_grouped", align_bytes=64)
+        dealt_words = keep.tile([P, S], U32, name="dealt_words", align_bytes=64)
         nc.vector.tensor_copy(
             dealt_words[:].rearrange("p (d c i) -> p c d i", d=D, i=4),
             picked_words[:].rearrange("p (c i d) -> p c d i", d=D, i=4),
@@ -153,9 +156,8 @@ def tile_picked_yimlsq_nrm_p_kernel(
         fx = [keep.tile([P, S], F32, name="fx%d" % t, align_bytes=64) for t in range(PACK)]
         we0 = [keep.tile([P, S], F32, name="we0_%d" % t) for t in range(PACK)]
         wf = [keep.tile([P, S], F32, name="wf%d" % t) for t in range(PACK)]
-        tanh_nm = [keep.tile([P, 2 * V], F32, name="tanh_nm%d" % i) for i in range(2)]
+        tanh_nm = [off_sb[PACK - 1][:, i * HALF : (i + 1) * HALF] for i in range(2)]
         work = [keep.tile([P, S], F32, name="work%d" % t) for t in range(PACK)]
-        sums0 = {}
 
         def offsets_of(c):
             t, vh = chunks[c]
@@ -187,9 +189,8 @@ def tile_picked_yimlsq_nrm_p_kernel(
             )
 
         def first_sums(t):
-            sums0[t] = psum.tile([P, 2 * V], F32, name="sums0", tag="bank%d" % (6, 7, 0, 1)[t])
-            group_sums(sums0[t], 0, we0[t], whole)
-            group_sums(sums0[t], V, wf[t], whole)
+            group_sums(weight_sums0[t], 0, we0[t], whole)
+            group_sums(value_sums0[t], 0, wf[t], whole)
 
         def normals(w2_codes, w2_scales):
             for i in range(2):
@@ -205,42 +206,56 @@ def tile_picked_yimlsq_nrm_p_kernel(
                             start=(d == 0),
                             stop=(d == D - 1),
                         )
-                nc.scalar.activation(out=tanh_nm[i][:], in_=bank[:], func=ACT.Tanh, scale=1.0 / D)
+                nc.scalar.activation(out=tanh_nm[i], in_=bank[:], func=ACT.Tanh, scale=1.0 / D)
 
-        for c in range(len(chunks)):
-            offsets_of(c)
         w2_grouped = round_weight(w2_raw, "w2_grouped", 1.0)
         w2_codes, w2_scales = quantize(w2_grouped, "w2")
-        for t, cells in [(0, halves[0]), (0, halves[1]), (1, whole), (2, whole), (3, halves[0]), (3, halves[1])]:
-            if t == 3 and cells.start == 0:
+        for t in range(PACK + 2):
+            if t < PACK:
+                offsets_of(2 * t)
+                offsets_of(2 * t + 1)
+            if t == PACK:
                 normals(w2_codes, w2_scales)
-            first_weights(t, cells)
-        for t, cells in [(t, whole) for t in range(PACK)]:
-            weighted_offsets(t, cells)
-        for t in range(3):
-            first_sums(t)
+            if 1 <= t <= PACK:
+                for cells in (halves if t - 1 in (0, PACK - 1) else [whole]):
+                    first_weights(t - 1, cells)
+            if t >= 2 and t - 2 < PACK:
+                weighted_offsets(t - 2, whole)
+        weights01 = psum.tile([P, 2 * V], F32, name="weights01", tag="bank6")
+        values01 = psum.tile([P, 2 * V], F32, name="values01", tag="bank7")
+        sums2 = psum.tile([P, 2 * V], F32, name="sums2", tag="bank0")
+        weight_sums0 = [weights01[:, 0:V], weights01[:, V : 2 * V], sums2[:, 0:V]]
+        value_sums0 = [values01[:, 0:V], values01[:, V : 2 * V], sums2[:, V : 2 * V]]
+        for t in range(2):
+            group_sums(weight_sums0[t], 0, we0[t], whole)
+        for t in range(2):
+            group_sums(value_sums0[t], 0, wf[t], whole)
+        first_sums(2)
 
-        def group_mean(weight_sums, value_sums, squared, inverse, turned):
-            width = inverse.shape[1]
+        def inverse_weight(weight_sums, squared, inverse):
             nc.scalar.activation(out=squared, in_=weight_sums, func=ACT.Square, bias=0.1)
             nc.scalar.activation(out=inverse, in_=squared, func=ACT.Abs_reciprocal_sqrt)
-            mean = ring.tile([P, width], F32, name="mean", tag="mean")
-            nc.vector.tensor_tensor(out=mean[:], in0=value_sums, in1=inverse, op=ALU.mult)
-            for s in range(width // P):
+
+        def turn(turned, mean):
+            for s in range(mean.shape[1] // P):
                 nc.tensor.transpose(turned[:, s * P : (s + 1) * P], mean[:, s * P : (s + 1) * P], ident[:])
 
         scaled = [keep.tile([P, S], F32, name="scaled%d" % t) for t in range(PACK)]
         m0 = {}
         m1 = {}
+        windows = [scaled[2], scaled[3], we0[3], scaled[0]]
         weight_sums1 = {}
         value_sums1 = {}
         picked_hid = keep.tile([P, PACK, U], BF16, name="picked_hid")
 
-        def first_mean(t):
-            m0[t] = psum.tile([P, V], F32, name="m0_%d" % t, tag="bank%d" % (2 + t))
-            first = t * V
-            squared = ring.tile([P, V], F32, name="squared", tag="squared")
-            group_mean(sums0[t][:, 0:V], sums0[t][:, V : 2 * V], squared[:], work[PACK - 1][:, first : first + V], m0[t])
+        def first_means(tiles, weight_sums, value_sums, squared):
+            inverse = work[PACK - 1][:, tiles[0] * V : (tiles[-1] + 1) * V]
+            inverse_weight(weight_sums, squared, inverse)
+            mean = keep.tile([P, len(tiles) * V], F32, name="mean0_%d" % tiles[0])
+            nc.vector.tensor_tensor(out=mean[:], in0=value_sums, in1=inverse, op=ALU.mult)
+            for i, t in enumerate(tiles):
+                m0[t] = psum.tile([P, V], F32, name="m0_%d" % t, tag="bank%d" % (2 + t))
+                turn(m0[t], mean[:, i * V : (i + 1) * V])
 
         def scale_weights(t):
             nc.vector.tensor_tensor(
@@ -260,63 +275,106 @@ def tile_picked_yimlsq_nrm_p_kernel(
             nc.scalar.activation(out=inverse, in_=paired_by_point(work[t], cells), func=ACT.Square)
             nc.scalar.activation(out=inverse, in_=inverse, func=ACT.Abs_reciprocal_sqrt)
 
-        def second_sums(t, cells):
-            if cells.start == 0:
-                weight_sums1[t] = psum.tile([P, V], F32, name="s1_%d" % t, tag="bank%d" % (6 * (t % 2)))
-                value_sums1[t] = psum.tile([P, V], F32, name="n1_%d" % t, tag="bank%d" % (6 * (t % 2) + 1))
+        def second_weights(t, cells):
             we1 = by_point(we0[t], cells)
             nc.vector.tensor_tensor(out=we1, in0=paired_by_point(scaled[t], cells), in1=we1, op=ALU.mult)
-            nc.vector.tensor_tensor(out=by_point(wf[t], cells), in0=we1, in1=paired_by_point(fx[t], cells), op=ALU.mult)
+
+        def second_values(t, cells):
+            nc.vector.tensor_tensor(
+                out=by_point(wf[t], cells), in0=by_point(we0[t], cells), in1=paired_by_point(fx[t], cells), op=ALU.mult
+            )
+
+        def second_sums(t, cells):
+            if cells.start == 0:
+                weight_sums1[t] = psum.tile([P, V], F32, name="s1_%d" % t, tag="bank%d" % (6 - 6 * (t % 2)))
+                value_sums1[t] = psum.tile([P, V], F32, name="n1_%d" % t, tag="bank%d" % (7 - 6 * (t % 2)))
+            second_weights(t, cells)
+            second_values(t, cells)
             group_sums(weight_sums1[t], 0, we0[t], cells)
             group_sums(value_sums1[t], 0, wf[t], cells)
 
-        def hidden(t, cells):
-            if t < PACK - 1:
-                if cells.stop < V:
-                    return
-                cells = whole
-            if cells.start == 0:
-                m1[t] = psum.tile([P, V], F32, name="m1_%d" % t, tag="bank%d" % (2 + t))
+        def tanh_of(t, cells):
+            return tanh_nm[t // 2][:, (t % 2) * V + cells.start : (t % 2) * V + cells.stop]
+
+        def second_mean(t, cells, squared, mean):
             inverse = ring.tile([P, cells.stop - cells.start], F32, name="inverse", tag="inverse")
-            if t == PACK - 1:
-                squared = picked_hid[:, PACK - 2, :].bitcast(F32)[:, cells]
-            else:
-                squared = ring.tile([P, V], F32, name="squared", tag="squared")[:]
-            group_mean(weight_sums1[t][:, cells], value_sums1[t][:, cells], squared, inverse[:], m1[t][:, cells])
+            inverse_weight(weight_sums1[t][:, cells], squared, inverse[:])
+            nc.vector.tensor_tensor(out=mean, in0=value_sums1[t][:, cells], in1=inverse[:], op=ALU.mult)
+            m1[t] = psum.tile([P, cells.stop - cells.start], F32, name="m1_%d" % t, tag="bank%d" % (2 + t))
+            turn(m1[t], mean)
+
+        def hidden(t, cells):
             nc.vector.scalar_tensor_tensor(
-                out=scaled[t][:, cells],
-                in0=m1[t][:, cells],
+                out=windows[t][:, cells],
+                in0=m1[t][:],
                 scalar=unit_sb[:, t : t + 1],
-                in1=tanh_nm[t // 2][:, (t % 2) * V + cells.start : (t % 2) * V + cells.stop],
+                in1=tanh_of(t, cells),
+                op0=ALU.mult,
+                op1=ALU.mult,
+            )
+
+        def last_cells(t, cells, squared):
+            def over_points(rows):
+                return rows[:].rearrange("p (d v) -> p v d", d=D)[:, cells, :]
+
+            width = cells.stop - cells.start
+            second_weights(t, cells)
+            weight_sum = keep.tile([P, width], F32, name="weight_sum")
+            nc.vector.tensor_reduce(out=weight_sum[:], in_=over_points(we0[t]), axis=AXIS.X, op=ALU.add)
+            second_values(t, cells)
+            hidden(t - 1, whole)
+            second_mean(t, halves[0], last_squares[:, halves[0]], fx[t][:, V : V + VH])
+            inverse = keep.tile([P, width], F32, name="last_inverse")
+            inverse_weight(weight_sum[:], squared, inverse[:])
+            value_sum = keep.tile([P, width], F32, name="value_sum")
+            nc.vector.tensor_reduce(out=value_sum[:], in_=over_points(wf[t]), axis=AXIS.X, op=ALU.add)
+            nc.vector.tensor_tensor(out=inverse[:], in0=inverse[:], in1=tanh_of(t, cells), op=ALU.mult)
+            nc.vector.scalar_tensor_tensor(
+                out=windows[t][:, cells],
+                in0=value_sum[:],
+                scalar=unit_sb[:, t : t + 1],
+                in1=inverse[:],
                 op0=ALU.mult,
                 op1=ALU.mult,
             )
 
         def look_up(t, queries, on_vector):
-            window = scaled[t][:].indirect(qry_sb[:, queries.start // LIST_COLS : queries.stop // LIST_COLS])
+            window = windows[t][:].indirect(qry_sb[:, queries.start // LIST_COLS : queries.stop // LIST_COLS])
             if on_vector:
                 nc.vector.tensor_copy(picked_hid[:, t, queries], window)
             else:
                 nc.scalar.activation(out=picked_hid[:, t, queries], in_=window, func=ACT.Copy)
 
-        steps = [(t, whole) for t in range(PACK - 1)] + [(PACK - 1, halves[0]), (PACK - 1, halves[1])]
-        for t in range(2):
-            first_mean(t)
-        first_sums(PACK - 1)
-        for step in range(len(steps) + 2 + 1):
+        squares = keep.tile([P, 2 * V], F32, name="squares")
+        first_means([0, 1], weights01[:], values01[:], squares[:, 0 : 2 * V])
+        last_squares = picked_hid[:, PACK - 2, :].bitcast(F32)
+        steps = [(0, halves[0]), (0, halves[1]), (1, whole), (2, whole), (3, halves[0]), (3, halves[1])]
+        for step in range(len(steps) + 1):
             if step < len(steps):
-                if steps[step][0] not in m0:
-                    first_mean(steps[step][0])
                 residual(*steps[step])
+            if step == 1:
+                first_means([2], weight_sums0[2], value_sums0[2], work[PACK - 1][:, 0:V])
+                sums3 = psum.tile([P, 2 * V], F32, name="sums3", tag="bank0")
+                weight_sums0.append(sums3[:, 0:V])
+                value_sums0.append(sums3[:, V : 2 * V])
+                first_sums(PACK - 1)
             if step == 0:
                 for t in range(PACK):
                     scale_weights(t)
             if 0 <= step - 1 < len(steps):
-                denominators(*steps[step - 1])
-            if 0 <= step - 2 - 1 < len(steps):
-                hidden(*steps[step - 2 - 1])
-            if 0 <= step - 2 < len(steps):
-                second_sums(*steps[step - 2])
+                t, cells = steps[step - 1]
+                denominators(t, cells)
+                if step == 2:
+                    first_means([3], weight_sums0[3], value_sums0[3], work[0][:, (2 - 1) * V : 2 * V])
+            if 0 <= step - 1 < len(steps) - 1:
+                t, cells = steps[step - 1]
+                second_sums(t, cells)
+                if t >= 2:
+                    hidden(t - 2, whole)
+                if t >= 1:
+                    second_mean(t - 1, whole, work[t - 1][:, V : 2 * V], fx[t][:, 0:V])
+        last_cells(PACK - 1, halves[1], last_squares[:, halves[1]])
+        hidden(PACK - 1, halves[0])
         for t, first, count, on_vector in [(t, 256 * h, 256, False) for t in range(3) for h in range(2)] + [(3, 0, 128, True), (3, 128, 128, False), (3, 256, 256, False)]:
             look_up(t, slice(first, first + count), on_vector)
 

from contextlib import ExitStack

import concourse.mybir as mybir
from concourse.masks import make_identity

FLOPS = 1140850688

F32 = mybir.dt.float32
BF16 = mybir.dt.bfloat16
I32 = mybir.dt.int32
U32 = mybir.dt.uint32
U16 = mybir.dt.uint16
U8 = mybir.dt.uint8
FP8X4 = mybir.dt.float8_e4m3fn_x4
ACT = mybir.ActivationFunctionType
ALU = mybir.AluOpType
AXIS = mybir.AxisListType

P = 128
PACK = 4
K, T, S, D, N, H, V, U = 512, 2048, 1024, 4, 128, 512, 256, 512
HALF = S // 2
VH = V // 2
QUERY_SLICE = 128
LIST_COLS = 16
W1_PIECES = 2
WEIGHT_BANKS = ("bank7", "bank2")
VALUE_BANKS = ("bank6", "bank3")


def tile_picked_yimlsq_nrm_p_kernel(
    tc, x_words, x_scales, w1, w2, off, sg, unit, w3, offs, qry, out
):
    nc = tc.nc
    with ExitStack() as ctx:
        lists = ctx.enter_context(tc.tile_pool(name="lists", bufs=1))
        keep = ctx.enter_context(tc.tile_pool(name="keep", bufs=1))
        ring = ctx.enter_context(tc.tile_pool(name="ring", bufs=3))
        psum = ctx.enter_context(tc.psum_pool(name="psum", bufs=1))

        offs_sb = lists.tile([P, S // LIST_COLS], U16, name="offs_sb")
        qry_sb = lists.tile([P, U // LIST_COLS], U16, name="qry_sb")

        table_words = keep.tile([P, T], I32, name="table_words")
        table_scales = keep.tile([P, T], U8, name="table_scales")
        nc.vector.memset(table_scales[:].bitcast(I32), 0)

        def load_weight_piece(w, i, pieces, name):
            width = H // pieces
            raw = keep.tile([P, PACK, width], F32, name="%s%d" % (name, i), align_bytes=64)
            nc.sync.dma_start(raw[:], w.rearrange("(p j) c -> p j c", j=PACK)[:, :, i * width : (i + 1) * width])
            return raw

        def load_rows(rows, src, t, cols):
            nc.sync.dma_start(rows[:, cols], src.rearrange("(p t) s -> p t s", t=PACK)[:, t, cols])

        off_sb = [keep.tile([P, S], F32, name="off%d" % t) for t in range(PACK)]
        nc.sync.dma_start(offs_sb[:], offs)
        nc.sync.dma_start(qry_sb[:], qry)
        for q in range(4):
            nc.sync.dma_start(
                table_scales[32 * q : 32 * q + 4, :].bitcast(I32), x_scales[0][4 * q : 4 * q + 4, :].bitcast(I32)
            )
        nc.sync.dma_start(table_words[:], x_words[0].rearrange("p c r -> p (c r)").bitcast(I32))
        w1_raw = [load_weight_piece(w1, i, W1_PIECES, "w1_raw") for i in range(W1_PIECES)]
        w2_raw = []
        for what, i in [("w2",0),("half",0),("w2",1),("half",1),("off",1),("off",2),("off",3)]:
            if what == "w2":
                w2_raw.append(load_weight_piece(w2, i, 2, "w2_raw"))
            elif what == "half":
                load_rows(off_sb[0], off, 0, slice(i * HALF, (i + 1) * HALF))
            else:
                load_rows(off_sb[i], off, i, slice(0, S))
        sg_sb = [keep.tile([P, S], F32, name="sg%d" % t) for t in range(PACK)]
        for t in range(PACK):
            load_rows(sg_sb[t], sg, t, slice(0, S))
        w3_raw = keep.tile([P, PACK, N], F32, name="w3_raw")
        nc.sync.dma_start(w3_raw[:], w3.rearrange("(p j) n -> p j n", j=PACK))
        unit_sb = keep.tile([P, PACK], F32, name="unit_sb")
        nc.sync.dma_start(unit_sb[:], unit.rearrange("(p t) o -> p (t o)", t=PACK))

        ident = keep.tile([P, P], F32, name="ident")
        make_identity(nc, ident[:])

        def round_weight(raw, name, factor):
            grouped = keep.tile([P, PACK, P, PACK], BF16, name=name, align_bytes=64)
            width = P // len(raw)
            for i in range(len(raw)):
                dst = grouped[:, :, i * width : (i + 1) * width, :].rearrange("p t m j -> p m t j")
                src = raw[i][:].rearrange("p j (m t) -> p m t j", t=PACK)
                nc.scalar.activation(out=dst, in_=src, func=ACT.Copy, scale=factor)
            return grouped[:].rearrange("p t m j -> p (t m j)")

        def quantize(grouped, name):
            width = grouped.shape[1] // PACK
            codes = keep.tile([P, width], U32, name=name + "_codes", align_bytes=64)
            scales = keep.tile([P, width], U8, name=name + "_scales", align_bytes=64)
            nc.vector.quantize_mx(out=codes[:].bitcast(FP8X4), scales=scales[:], in_=grouped)
            return codes, scales

        picked_scales = keep.tile([P, S], U8, name="picked_scales", align_bytes=64)
        nc.vector.tensor_copy(picked_scales[:], table_scales[:].indirect(offs_sb[:]))
        picked_words = keep.tile([P, S], U32, name="picked_words", align_bytes=64)
        for vh in range(2):
            cols = HALF // LIST_COLS
            nc.vector.tensor_copy(
                picked_words[:, vh * HALF : (vh + 1) * HALF],
                table_words[:].bitcast(U32).indirect(offs_sb[:, vh * cols : (vh + 1) * cols]),
            )
        w1_codes, w1_scales = quantize(round_weight(w1_raw, "w1_grouped", -0.5), "w1")
        dealt_scales = keep.tile([P, S], U8, name="dealt_scales", align_bytes=64)
        nc.vector.tensor_copy(
            dealt_scales[:].rearrange("p (d v) -> p d v", d=D), picked_scales[:].rearrange("p (v d) -> p d v", d=D)
        )
        dealt_words = keep.tile([P, S], U32, name="dealt_words", align_bytes=64)
        nc.vector.tensor_copy(
            dealt_words[:].rearrange("p (d c i) -> p c d i", d=D, i=4),
            picked_words[:].rearrange("p (c i d) -> p c d i", d=D, i=4),
        )

        def feature_cols(t):
            return slice(t * P, (t + 1) * P)

        def paired(rows, cells):
            return rows[:].rearrange("p (a v b) -> p a v b", a=2, b=2)[:, :, cells, :]

        def listed(rows, cells):
            return rows[:].rearrange("p (v a b) -> p a v b", a=2, b=2)[:, :, cells, :]

        def paired_by_point(rows, cells):
            return rows[:].rearrange("p (a v b) -> p a b v", a=2, b=2)[:, :, :, cells]

        def by_point(rows, cells):
            return rows[:].rearrange("p (a b v) -> p a b v", a=2, b=2)[:, :, :, cells]

        def by_point_paired(rows, cells):
            return rows[:].rearrange("p (a b v) -> p a v b", a=2, b=2)[:, :, cells, :]

        def group_sums(bank, first_col, values, cells):
            for v0 in range(cells.start, cells.stop, P):
                for d in range(D):
                    nc.tensor.matmul(
                        bank[:, first_col + v0 : first_col + v0 + P],
                        lhsT=values[:, d * V + v0 : d * V + v0 + P],
                        rhs=ident[:],
                        is_transpose=True,
                        start=(d == 0),
                        stop=(d == D - 1),
                    )

        halves = [slice(0, VH), slice(VH, V)]
        whole = slice(0, V)
        chunks = [(t, vh) for t in range(PACK) for vh in range(2)]
        last = len(chunks) - 1

        fx = [keep.tile([P, S], F32, name="fx%d" % t, align_bytes=64) for t in range(PACK)]
        we0 = [keep.tile([P, S], F32, name="we0_%d" % t) for t in range(PACK)]
        wf = [keep.tile([P, S], F32, name="wf%d" % t) for t in range(PACK)]
        tanh_nm = [off_sb[PACK - 1][:, i * HALF : (i + 1) * HALF] for i in range(2)]
        work = [keep.tile([P, S], F32, name="work%d" % t) for t in range(PACK)]

        def offsets_of(c):
            t, vh = chunks[c]
            py = psum.tile([P, HALF], F32, name="py%d" % c, tag="bank%d" % (c % 4))
            nc.tensor.matmul_mx(
                py[:],
                lhsT=w1_codes[:, feature_cols(t)].bitcast(FP8X4),
                lhsT_scale=w1_scales[:, feature_cols(t)],
                rhs=picked_words[:, vh * HALF : (vh + 1) * HALF].bitcast(FP8X4),
                rhs_scale=picked_scales[:, vh * HALF : (vh + 1) * HALF],
                start=True,
                stop=True,
            )
            nc.vector.tensor_tensor(
                out=paired(fx[t], halves[vh]),
                in0=listed(py, slice(0, VH)),
                in1=listed(off_sb[t], halves[vh]),
                op=ALU.add,
            )

        def first_weights(t, cells):
            square = by_point(work[t], cells)
            nc.scalar.activation(out=square, in_=paired_by_point(fx[t], cells), func=ACT.Square, scale=0.6)
            nc.scalar.activation(out=by_point(we0[t], cells), in_=square, func=ACT.Exp, scale=-1.0)

        def weighted_offsets(t, cells):
            nc.vector.tensor_tensor(
                out=by_point(wf[t], cells), in0=by_point(we0[t], cells), in1=paired_by_point(fx[t], cells), op=ALU.mult
            )

        def first_sums(t):
            group_sums(weight_sums0[t], 0, we0[t], whole)
            group_sums(value_sums0[t], 0, wf[t], whole)

        def normals(w2_codes, w2_scales):
            for i in range(2):
                bank = psum.tile([P, 2 * V], F32, name="normal%d" % i, tag="bank%d" % (4 + i))
                for t in (2 * i, 2 * i + 1):
                    for d in range(D):
                        nc.tensor.matmul_mx(
                            bank[:, (t % 2) * V : (t % 2 + 1) * V],
                            lhsT=w2_codes[:, feature_cols(t)].bitcast(FP8X4),
                            lhsT_scale=w2_scales[:, feature_cols(t)],
                            rhs=dealt_words[:, d * V : (d + 1) * V].bitcast(FP8X4),
                            rhs_scale=dealt_scales[:, d * V : (d + 1) * V],
                            start=(d == 0),
                            stop=(d == D - 1),
                        )
                nc.scalar.activation(out=tanh_nm[i], in_=bank[:], func=ACT.Tanh, scale=1.0 / D)

        w2_grouped = round_weight(w2_raw, "w2_grouped", 1.0)
        w2_codes, w2_scales = quantize(w2_grouped, "w2")
        for t in range(PACK + 2):
            if t < PACK:
                offsets_of(2 * t)
                offsets_of(2 * t + 1)
            if t == PACK:
                normals(w2_codes, w2_scales)
            if 1 <= t <= PACK:
                for cells in (halves if t - 1 in (0, PACK - 1) else [whole]):
                    first_weights(t - 1, cells)
            if t >= 2 and t - 2 < PACK:
                weighted_offsets(t - 2, whole)
        weights01 = psum.tile([P, 2 * V], F32, name="weights01", tag="bank6")
        values01 = psum.tile([P, 2 * V], F32, name="values01", tag="bank7")
        sums2 = psum.tile([P, 2 * V], F32, name="sums2", tag="bank0")
        weight_sums0 = [weights01[:, 0:V], weights01[:, V : 2 * V], sums2[:, 0:V]]
        value_sums0 = [values01[:, 0:V], values01[:, V : 2 * V], sums2[:, V : 2 * V]]
        for t in range(2):
            group_sums(weight_sums0[t], 0, we0[t], whole)
        for t in range(2):
            group_sums(value_sums0[t], 0, wf[t], whole)
        first_sums(2)

        def inverse_weight(weight_sums, squared, inverse):
            nc.scalar.activation(out=squared, in_=weight_sums, func=ACT.Square, bias=0.1)
            nc.scalar.activation(out=inverse, in_=squared, func=ACT.Abs_reciprocal_sqrt)

        def turn(turned, mean):
            for s in range(mean.shape[1] // P):
                nc.tensor.transpose(turned[:, s * P : (s + 1) * P], mean[:, s * P : (s + 1) * P], ident[:])

        scaled = [keep.tile([P, S], F32, name="scaled%d" % t) for t in range(PACK)]
        m0 = {}
        m1 = {}
        windows = [scaled[2], scaled[3], we0[3], scaled[0]]
        weight_sums1 = {}
        value_sums1 = {}
        picked_hid = keep.tile([P, PACK, U], BF16, name="picked_hid")

        def first_means(tiles, weight_sums, value_sums, squared):
            inverse = work[PACK - 1][:, tiles[0] * V : (tiles[-1] + 1) * V]
            inverse_weight(weight_sums, squared, inverse)
            mean = keep.tile([P, len(tiles) * V], F32, name="mean0_%d" % tiles[0])
            nc.vector.tensor_tensor(out=mean[:], in0=value_sums, in1=inverse, op=ALU.mult)
            for i, t in enumerate(tiles):
                m0[t] = psum.tile([P, V], F32, name="m0_%d" % t, tag="bank%d" % (2 + t))
                turn(m0[t], mean[:, i * V : (i + 1) * V])

        def scale_weights(t):
            nc.vector.tensor_tensor(
                out=paired(scaled[t], whole), in0=by_point_paired(we0[t], whole), in1=listed(sg_sb[t], whole), op=ALU.mult
            )

        def residual(t, cells):
            res = paired(work[t], cells)
            spread = m0[t][:, cells].unsqueeze(1).unsqueeze(3).to_broadcast([P, 2, cells.stop - cells.start, 2])
            nc.vector.tensor_tensor(out=res, in0=paired(fx[t], cells), in1=spread, op=ALU.subtract)
            nc.scalar.activation(out=res, in_=res, func=ACT.Abs)

        def denominators(t, cells):
            denom = paired(work[t], cells)
            nc.vector.tensor_tensor(out=denom, in0=denom, in1=listed(sg_sb[t], cells), op=ALU.add)
            inverse = by_point(we0[t], cells)
            nc.scalar.activation(out=inverse, in_=paired_by_point(work[t], cells), func=ACT.Square)
            nc.scalar.activation(out=inverse, in_=inverse, func=ACT.Abs_reciprocal_sqrt)

        def second_weights(t, cells):
            we1 = by_point(we0[t], cells)
            nc.vector.tensor_tensor(out=we1, in0=paired_by_point(scaled[t], cells), in1=we1, op=ALU.mult)

        def second_values(t, cells):
            nc.vector.tensor_tensor(
                out=by_point(wf[t], cells), in0=by_point(we0[t], cells), in1=paired_by_point(fx[t], cells), op=ALU.mult
            )

        def second_sums(t, cells):
            if cells.start == 0:
                weight_sums1[t] = psum.tile([P, V], F32, name="s1_%d" % t, tag="bank%d" % (6 - 6 * (t % 2)))
                value_sums1[t] = psum.tile([P, V], F32, name="n1_%d" % t, tag="bank%d" % (7 - 6 * (t % 2)))
            second_weights(t, cells)
            second_values(t, cells)
            group_sums(weight_sums1[t], 0, we0[t], cells)
            group_sums(value_sums1[t], 0, wf[t], cells)

        def tanh_of(t, cells):
            return tanh_nm[t // 2][:, (t % 2) * V + cells.start : (t % 2) * V + cells.stop]

        def second_mean(t, cells, squared, mean):
            inverse = ring.tile([P, cells.stop - cells.start], F32, name="inverse", tag="inverse")
            inverse_weight(weight_sums1[t][:, cells], squared, inverse[:])
            nc.vector.tensor_tensor(out=mean, in0=value_sums1[t][:, cells], in1=inverse[:], op=ALU.mult)
            m1[t] = psum.tile([P, cells.stop - cells.start], F32, name="m1_%d" % t, tag="bank%d" % (2 + t))
            turn(m1[t], mean)

        def hidden(t, cells):
            nc.vector.scalar_tensor_tensor(
                out=windows[t][:, cells],
                in0=m1[t][:],
                scalar=unit_sb[:, t : t + 1],
                in1=tanh_of(t, cells),
                op0=ALU.mult,
                op1=ALU.mult,
            )

        def last_cells(t, cells, squared):
            def over_points(rows):
                return rows[:].rearrange("p (d v) -> p v d", d=D)[:, cells, :]

            width = cells.stop - cells.start
            second_weights(t, cells)
            weight_sum = keep.tile([P, width], F32, name="weight_sum")
            nc.vector.tensor_reduce(out=weight_sum[:], in_=over_points(we0[t]), axis=AXIS.X, op=ALU.add)
            second_values(t, cells)
            hidden(t - 1, whole)
            second_mean(t, halves[0], last_squares[:, halves[0]], fx[t][:, V : V + VH])
            inverse = keep.tile([P, width], F32, name="last_inverse")
            inverse_weight(weight_sum[:], squared, inverse[:])
            value_sum = keep.tile([P, width], F32, name="value_sum")
            nc.vector.tensor_reduce(out=value_sum[:], in_=over_points(wf[t]), axis=AXIS.X, op=ALU.add)
            nc.vector.tensor_tensor(out=inverse[:], in0=inverse[:], in1=tanh_of(t, cells), op=ALU.mult)
            nc.vector.scalar_tensor_tensor(
                out=windows[t][:, cells],
                in0=value_sum[:],
                scalar=unit_sb[:, t : t + 1],
                in1=inverse[:],
                op0=ALU.mult,
                op1=ALU.mult,
            )

        def look_up(t, queries, on_vector):
            window = windows[t][:].indirect(qry_sb[:, queries.start // LIST_COLS : queries.stop // LIST_COLS])
            if on_vector:
                nc.vector.tensor_copy(picked_hid[:, t, queries], window)
            else:
                nc.scalar.activation(out=picked_hid[:, t, queries], in_=window, func=ACT.Copy)

        squares = keep.tile([P, 2 * V], F32, name="squares")
        first_means([0, 1], weights01[:], values01[:], squares[:, 0 : 2 * V])
        last_squares = picked_hid[:, PACK - 2, :].bitcast(F32)
        steps = [(0, halves[0]), (0, halves[1]), (1, whole), (2, whole), (3, halves[0]), (3, halves[1])]
        for step in range(len(steps) + 1):
            if step < len(steps):
                residual(*steps[step])
            if step == 1:
                first_means([2], weight_sums0[2], value_sums0[2], work[PACK - 1][:, 0:V])
                sums3 = psum.tile([P, 2 * V], F32, name="sums3", tag="bank0")
                weight_sums0.append(sums3[:, 0:V])
                value_sums0.append(sums3[:, V : 2 * V])
                first_sums(PACK - 1)
            if step == 0:
                for t in range(PACK):
                    scale_weights(t)
            if 0 <= step - 1 < len(steps):
                t, cells = steps[step - 1]
                denominators(t, cells)
                if step == 2:
                    first_means([3], weight_sums0[3], value_sums0[3], work[0][:, (2 - 1) * V : 2 * V])
            if 0 <= step - 1 < len(steps) - 1:
                t, cells = steps[step - 1]
                second_sums(t, cells)
                if t >= 2:
                    hidden(t - 2, whole)
                if t >= 1:
                    second_mean(t - 1, whole, work[t - 1][:, V : 2 * V], fx[t][:, 0:V])
        last_cells(PACK - 1, halves[1], last_squares[:, halves[1]])
        hidden(PACK - 1, halves[0])
        for t, first, count, on_vector in [(t, 256 * h, 256, False) for t in range(3) for h in range(2)] + [(3, 0, 128, True), (3, 128, 128, False), (3, 256, 256, False)]:
            look_up(t, slice(first, first + count), on_vector)

        w3_grouped = keep.tile([P, N, PACK], BF16, name="w3_grouped", tag="fx0", align_bytes=64)
        nc.scalar.activation(out=w3_grouped[:], in_=w3_raw[:].rearrange("p j n -> p n j"), func=ACT.Copy)
        w3_codes, w3_scales = quantize(w3_grouped[:].rearrange("p n j -> p (n j)"), "w3")
        for h in range(2):
            queries = slice(h * (U // 2), (h + 1) * (U // 2))
            hid = keep.tile([P, U // 2, PACK], BF16, name="hid%d" % h, align_bytes=64)
            nc.vector.tensor_copy(
                hid[:].rearrange("p (c i) t -> p c t i", i=4),
                picked_hid[:, :, queries].rearrange("p t (c i) -> p c t i", i=4),
            )
            hid_codes, hid_scales = quantize(hid[:].rearrange("p r t -> p (r t)"), "hid%d" % h)
            patches = psum.tile([P, U // 2], F32, name="patches%d" % h, tag="bank%d" % (2 + h))
            nc.tensor.matmul_mx(
                patches[:],
                lhsT=w3_codes[:].bitcast(FP8X4),
                lhsT_scale=w3_scales[:],
                rhs=hid_codes[:].bitcast(FP8X4),
                rhs_scale=hid_scales[:],
                start=True,
                stop=True,
            )
            result = keep.tile([P, U // 2], F32, name="result%d" % h)
            nc.scalar.copy(result[:], patches[:])
            nc.sync.dma_start(out[:, queries], result[:])
